import numpy as np
import ml_dtypes


def mxq(x, axis, fmt="e4m3"):
    dtype, down = {"e4m3": (ml_dtypes.float8_e4m3fn, 7), "e5m2": (ml_dtypes.float8_e5m2, 14)}[fmt]
    v = np.moveaxis(np.asarray(x, np.float32).astype(ml_dtypes.bfloat16).astype(np.float64), axis, -1)
    blocks = v.reshape(v.shape[:-1] + (-1, 32))
    amax = np.abs(blocks).max(-1, keepdims=True)
    byte = np.maximum(np.where(amax > 0, np.frexp(amax)[1] - 1 + 127, 0) - down, 1)
    scale = np.exp2(byte - 127.0)
    codes = (blocks / scale).astype(np.float32).astype(dtype).astype(np.float64)
    return np.moveaxis((codes * scale).reshape(v.shape), -1, axis)


WIDE = False


def mx_kscale(k):
    if not WIDE:
        return np.ones(k)
    levels = np.array([10, -10, 5, -5, 0])
    if k % 512:
        return np.exp2(np.random.permutation(np.resize(levels, k // 32))).repeat(32)
    a = np.empty((k // 512, 16))
    for p in range(k // 512):
        a[p, :8] = np.random.permutation(np.resize(levels, 8))
        for g in range(8):
            far = levels[np.abs(levels - a[p, g]) >= 10]
            a[p, g + 8] = far[np.random.randint(len(far))]
    return np.exp2(a.ravel()).repeat(32)


def f64(x):
    return np.asarray(x).astype(np.float64)


def striped(idx):
    return np.tile(idx.reshape(-1, 16).T, (8, 1)).astype(np.uint16)


def unstriped(offs):
    return offs[:16].T.reshape(-1).astype(np.int64)


def striped8(idx):
    return np.concatenate([x.reshape(-1, 16).T for x in idx]).astype(np.uint16)


def runs(offs, k):
    lists = np.stack([offs[16 * r : 16 * r + 16].T.reshape(-1) for r in range(8)]).astype(np.int64)
    return lists[np.arange(k) % 512 // 64]


def pack_weight(w):
    k, n = w.shape
    w = f64(np.asarray(w, np.float32).astype(ml_dtypes.bfloat16)).reshape(k // 32, 32, n)
    amax = np.abs(w).max(1)
    byte = np.clip(np.where(amax > 0, np.frexp(amax)[1] - 1 + 127 - 7, 1), 1, 254)
    scaled = (w * np.exp2(127.0 - byte)[:, None, :]).reshape(k, n).astype(np.float32)
    words = np.ascontiguousarray(scaled.reshape(k // 512, 128, 4, n).transpose(0, 1, 3, 2)).astype(ml_dtypes.float8_e4m3fn).view(np.uint8)
    return words, np.ascontiguousarray(byte.astype(np.uint8).reshape(k // 512, 16, n))


def unpack_weight(words, scales):
    g, p, n, _ = words.shape
    vals = np.ascontiguousarray(words).view(ml_dtypes.float8_e4m3fn).astype(np.float64) * np.repeat(np.exp2(scales.astype(np.float64) - 127.0), 8, axis=1)[..., None]
    return vals.transpose(0, 1, 3, 2).reshape(g * 512, n)

def planes(y):
    n, m = y.shape
    v = y.astype(np.float32).astype(ml_dtypes.bfloat16).astype(np.float64).reshape(n // 32, 32, m)
    top = np.abs(v).max(1)
    byte = np.clip(np.where(top > 0, np.frexp(top)[1] - 1 + 127 - 7, 1), 1, 254)
    codes = (v * np.exp2(127.0 - byte)[:, None, :]).reshape(n, m).astype(np.float32).astype(ml_dtypes.float8_e4m3fn).view(np.uint8)
    words = codes.reshape(n // 512, 128, 4, m).transpose(0, 1, 3, 2)
    return np.ascontiguousarray(words), np.ascontiguousarray(byte.astype(np.uint8).reshape(n // 512, 16, m))


K, T, S, N, G, H, W = 512, 1024, 512, 512, 2048, 512, 256


def setup_inputs():
    n = np.random.standard_normal
    s = mx_kscale(K)[:, None]
    u = mx_kscale(S)
    packed_xT = pack_weight(n((K, T)) * s)
    packed_dT = pack_weight(n((K, G)) / s)
    packed_w1 = pack_weight(n((H, N)) / np.sqrt(H) / u[:, None])
    perm = np.stack([np.random.permutation(S) for _ in range(8)])
    return {
        "x_words": packed_xT[0],
        "x_scales": packed_xT[1],
        "d_words": packed_dT[0],
        "d_scales": packed_dT[1],
        "gn": (np.random.uniform(0.5, 1.5, (H, 1)) * u[:, None]).astype(np.float32),
        "w1_words": packed_w1[0],
        "w1_scales": packed_w1[1],
        "offs": striped(np.random.permutation(T)[:S]),
        "k1": striped8(np.random.randint(0, G, (8, H))),
        "two": striped(np.random.permutation(T)[:S]),
        "k2": striped8(np.random.randint(0, G, (8, H))),
        "n1": striped8(np.stack([np.random.permutation(S) for _ in range(8)])),
        "n2": striped8(np.stack([np.random.permutation(S) for _ in range(8)])),
        "n3": striped8(np.stack([np.random.permutation(S) for _ in range(8)])),
        "n4": striped8(np.stack([np.random.permutation(S) for _ in range(8)])),
        "n5": striped8(perm[:, :W]),
        "n6": striped8(perm[:, W:]),
    }


def reference(x_words, x_scales, d_words, d_scales, gn, w1_words, w1_scales, offs, k1, two, k2, n1, n2, n3, n4, n5, n6):
    d_k1 = unpack_weight(d_words, d_scales)[np.arange(K)[:, None], runs(k1, K)]
    xq = unpack_weight(x_words, x_scales)[:, unstriped(offs)]
    a = 0.0625 * (d_k1.T @ xq)
    d_k2 = unpack_weight(d_words, d_scales)[np.arange(K)[:, None], runs(k2, K)]
    x_two = unpack_weight(x_words, x_scales)[:, unstriped(two)]
    b = 0.0625 * (d_k2.T @ x_two)
    z = f64(gn) * (np.maximum(a[np.arange(H)[:, None], runs(n1, H)] + b[np.arange(H)[:, None], runs(n3, H)], a[np.arange(H)[:, None], runs(n2, H)] + b[np.arange(H)[:, None], runs(n4, H)]))
    h = unpack_weight(w1_words, w1_scales).T @ mxq(z, 0, "e4m3")
    pa = h[np.arange(N)[:, None], runs(n5, N)]
    pb = h[np.arange(N)[:, None], runs(n6, N)]
    rb = pa - pb
    ra = 0.75 * (pa + pb)
    ds = np.zeros((N, S))
    ds[np.arange(N)[:, None], runs(n5, N)] = ra
    out = ds.copy()
    out[np.arange(N)[:, None], runs(n6, N)] = rb
    return (out,) + planes(out)

@@ -1,0 +1,253 @@
+from contextlib import ExitStack
+
+import concourse.mybir as mybir
+
+K, T, S, N, G, H, W = 512, 1024, 512, 512, 2048, 512, 256
+FLOPS = 3 * 2 * 512 * 512 * 512
+
+F32 = mybir.dt.float32
+BF16 = mybir.dt.bfloat16
+I32 = mybir.dt.int32
+U32 = mybir.dt.uint32
+U16 = mybir.dt.uint16
+U8 = mybir.dt.uint8
+FP8X4 = mybir.dt.float8_e4m3fn_x4
+ALU = mybir.AluOpType
+ACT = mybir.ActivationFunctionType
+COPY = ACT.Copy
+
+P = 128
+PACK = 4
+HALF = 256
+
+
+def tile_picked_twpqpathbhaar_none_po_kernel(
+    tc, x_words, x_scales, d_words, d_scales, gn, w1_words, w1_scales,
+    offs, k1, two, k2, n1, n2, n3, n4, n5, n6, out_0, out_1, out_2,
+):
+    nc = tc.nc
+    with ExitStack() as ctx:
+        lists = ctx.enter_context(tc.tile_pool(name="lists", bufs=1))
+        keep = ctx.enter_context(tc.tile_pool(name="keep", bufs=1))
+        psum = ctx.enter_context(tc.psum_pool(name="psum", bufs=1))
+
+        def load_list(name, dram):
+            tile = lists.tile(list(dram.shape), U16, name=name)
+            nc.sync.dma_start(tile[:], dram)
+            return tile
+
+        def load_words(name, dram):
+            tile = keep.tile([P, dram.shape[2]], U32, name=name, align_bytes=64)
+            nc.sync.dma_start(tile[:].bitcast(I32), dram[0].rearrange("p n r -> p (n r)").bitcast(I32))
+            return tile
+
+        def load_scale_window(name, dram):
+            tile = keep.tile([P, dram.shape[2]], U8, name=name, align_bytes=64)
+            nc.vector.memset(tile[:].bitcast(I32), 0)
+            nc.sync.dma_start(tile[0:P:8, :].bitcast(I32), dram[0].bitcast(I32))
+            return tile
+
+        k1_t = load_list("k1_t", k1)
+        ds_win = load_scale_window("ds_win", d_scales)
+        offs_t = load_list("offs_t", offs)
+        xs_win = load_scale_window("xs_win", x_scales)
+        xw_win = load_words("xw_win", x_words)
+        dw_win = load_words("dw_win", d_words)
+        k2_t = load_list("k2_t", k2)
+        two_t = load_list("two_t", two)
+        gain = keep.tile([P, PACK], F32, name="gain")
+        nc.sync.dma_start(gain[:], gn.rearrange("(p t) o -> p (t o)", t=PACK))
+        n1_t = load_list("n1_t", n1)
+        n2_t = load_list("n2_t", n2)
+        n3_t = load_list("n3_t", n3)
+        n4_t = load_list("n4_t", n4)
+        n5_t = load_list("n5_t", n5)
+        n6_t = load_list("n6_t", n6)
+
+        def deal(engine, dst, src, run):
+            engine.tensor_copy(
+                dst.rearrange("p (t c i) -> p c t i", t=PACK, i=run),
+                src.rearrange("p (c i t) -> p c t i", t=PACK, i=run),
+            )
+
+        def pick(name, d_list, x_list, queue):
+            ds = keep.tile([P, H], U8, name=name + "_ds", align_bytes=64)
+            xs = keep.tile([P, S], U8, name=name + "_xs", align_bytes=64)
+            planes = keep.tile([P, H + S], U8, name=name + "_planes", align_bytes=64)
+            nc.vector.tensor_copy(ds[:], ds_win[:].indirect(d_list[:]))
+            nc.vector.tensor_copy(xs[:], xs_win[:].indirect(x_list[:]))
+            deal(nc.vector, planes[:, 0:H], ds[:], 16)
+            nc.vector.tensor_copy(planes[:, H : H + S].bitcast(I32), xs[:].bitcast(I32))
+            for s in range(1, 4):
+                queue.dma_start(planes[s:P:32, :].bitcast(I32), planes[8 * s : P : 32, :].bitcast(I32))
+            xw = keep.tile([P, S], U32, name=name + "_xw", align_bytes=64)
+            dw = keep.tile([P, H], U32, name=name + "_dw", align_bytes=64)
+            dealt = keep.tile([P, H], U32, name=name + "_dealt", align_bytes=64)
+            nc.vector.tensor_copy(xw[:], xw_win[:].indirect(x_list[:]))
+            nc.vector.tensor_copy(dw[:], dw_win[:].indirect(d_list[:]))
+            deal(nc.vector, dealt[:].bitcast(I32), dw[:].bitcast(I32), 4)
+            return dealt, planes[:, 0:H], xw[:], planes[:, H : H + S]
+
+        def product(bank, t, lhs_words, lhs_plane, rhs_words, rhs_plane):
+            acc = psum.tile([P, rhs_words.shape[1]], F32, name="acc", tag="bank%d" % bank)
+            cols = slice(t * P, (t + 1) * P)
+            nc.tensor.matmul_mx(
+                out=acc[:], lhsT=lhs_words[:, cols].bitcast(FP8X4), lhsT_scale=lhs_plane[:, cols],
+                rhs=rhs_words.bitcast(FP8X4), rhs_scale=rhs_plane, start=True, stop=True,
+            )
+            return acc
+
+        size = keep.tile([P, PACK], F32, name="size")
+        sign = keep.tile([P, PACK], BF16, name="sign")
+        nc.scalar.activation(size[:], gain[:], ACT.Abs, scale=0.0625)
+        nc.scalar.activation(sign[:], gain[:], ACT.Sign)
+
+        a_ops = pick("a", k1_t, offs_t, nc.scalar)
+        a_acc = [product(t, t, *a_ops) for t in range(PACK)]
+        b_ops = pick("b", k2_t, two_t, nc.sync)
+        b_acc = [product(PACK + t, t, *b_ops) for t in range(PACK)]
+
+        w_raw = keep.tile([P, N], U32, name="w_raw", tag="a_dw", align_bytes=64)
+        nc.sync.dma_start(w_raw[:].bitcast(I32), w1_words[0].rearrange("p n r -> p (n r)").bitcast(I32))
+        ws_raw = keep.tile([P, N], U8, name="ws_raw", tag="a_xs", align_bytes=64)
+        nc.gpsimd.memset(ws_raw[:].bitcast(I32), 0)
+        for q in range(4):
+            nc.sync.dma_start(ws_raw[32 * q : 32 * q + 4, :].bitcast(I32), w1_scales[0, 4 * q : 4 * q + 4, :].bitcast(I32))
+        w_dealt = keep.tile([P, N], U32, name="w_dealt", align_bytes=64)
+        ws_dealt = keep.tile([P, N], U8, name="ws_dealt", align_bytes=64)
+        deal(nc.vector, w_dealt[:].bitcast(I32), w_raw[:].bitcast(I32), 4)
+        deal(nc.vector, ws_dealt[:], ws_raw[:], 16)
+
+        def evacuate(name, acc, t):
+            win = keep.tile([P, S], F32, name=name)
+            nc.scalar.activation(win[:], acc[:], COPY, scale=size[:, t : t + 1])
+            return win
+
+        from_a = [keep.tile([P, 2, PACK, HALF], F32, name="from_a%d" % h) for h in range(2)]
+        from_b = keep.tile([P, 2, PACK, HALF], F32, name="from_b")
+        sums = [keep.tile([P, 2, PACK, HALF], F32, name="sums%d" % h) for h in range(2)]
+        z_pairs = [keep.tile([P, 2, HALF, 2], BF16, name="z_pairs%d" % h, align_bytes=64) for h in range(2)]
+        z_bf = [keep.tile([P, HALF, 2, 2], BF16, name="z_bf%d" % h, align_bytes=64) for h in range(2)]
+        z_words = [keep.tile([P, HALF], U32, name="z_words%d" % h, align_bytes=64) for h in range(2)]
+        z_plane = [keep.tile([P, HALF], U8, name="z_plane%d" % h, align_bytes=64) for h in range(2)]
+        a_lists = (n1_t, n2_t)
+        b_lists = (n3_t, n4_t)
+
+        def fetch(dst, win, which, h, t):
+            for u in range(2):
+                nc.scalar.activation(dst[:, u, t, :], win[t][:].indirect(which[u][:, h * 16 : (h + 1) * 16]), COPY)
+
+        def fetch_b_and_add(h, t):
+            for u in range(2):
+                nc.vector.tensor_tensor(
+                    sums[h][:, u, t, :], b_win[t][:].indirect(b_lists[u][:, h * 16 : (h + 1) * 16]),
+                    from_a[h][:, u, t, :], ALU.add,
+                )
+
+        def add(h, t):
+            nc.vector.tensor_tensor(sums[h][:, :, t, :], from_b[:, :, t, :], from_a[h][:, :, t, :], ALU.add)
+
+        def larger(h, pair):
+            rows = slice(2 * pair, 2 * pair + 2)
+            nc.vector.tensor_tensor(
+                z_pairs[h][:, pair, :, :], sums[h][:, 0, rows, :].rearrange("p e j -> p j e"),
+                sums[h][:, 1, rows, :].rearrange("p e j -> p j e"), ALU.max,
+            )
+
+        def sign_z(h):
+            nc.vector.tensor_tensor(
+                z_bf[h][:], z_pairs[h][:].rearrange("p u j e -> p j u e"),
+                sign[:].rearrange("p (u e) -> p u e", e=2).unsqueeze(1).to_broadcast([P, HALF, 2, 2]), ALU.mult,
+            )
+
+        def quantise_z(h):
+            nc.vector.quantize_mx(
+                out=z_words[h][:].bitcast(FP8X4), scales=z_plane[h][:], in_=z_bf[h][:].rearrange("p j u e -> p (j u e)")
+            )
+            return [product(PACK * h + t, t, w_dealt, ws_dealt[:], z_words[h][:], z_plane[h][:]) for t in range(PACK)]
+
+        a_win = [evacuate("a_win%d" % t, a_acc[t], t) for t in range(PACK)]
+        fetch(from_a[0], a_win, a_lists, 0, 0)
+        fetch(from_a[0], a_win, a_lists, 0, 1)
+        b_win = [evacuate("b_win%d" % t, b_acc[t], t) for t in range(2)]
+        fetch(from_a[0], a_win, a_lists, 0, 2)
+        b_win.append(evacuate("b_win2", b_acc[2], 2))
+        fetch(from_a[0], a_win, a_lists, 0, 3)
+        b_win.append(evacuate("b_win3", b_acc[3], 3))
+        for t in range(PACK):
+            fetch(from_a[1], a_win, a_lists, 1, t)
+        for t in range(1, PACK):
+            fetch(from_b, b_win, b_lists, 1, t)
+
+        fetch_b_and_add(0, 0)
+        fetch_b_and_add(0, 1)
+        fetch_b_and_add(0, 2)
+        larger(0, 0)
+        fetch_b_and_add(0, 3)
+        fetch_b_and_add(1, 0)
+        larger(0, 1)
+        add(1, 1)
+        sign_z(0)
+        larger(1, 0)
+        h_acc = [quantise_z(0)]
+        add(1, 2)
+        add(1, 3)
+        larger(1, 1)
+        sign_z(1)
+        h_acc.append(quantise_z(1))
+
+        out_rows = out_0.rearrange("(p t) j -> p t j", t=PACK)
+        y_rows = keep.tile([P, PACK, S], BF16, name="y_rows", align_bytes=64)
+        placed = [keep.tile([P, S], F32, name="placed%d" % t) for t in range(PACK)]
+        h_win = [keep.tile([P, S], F32, name="h_win%d" % t) for t in range(PACK)]
+        parts = [keep.tile([P, 4, W], F32, name="part%d" % t) for t in range(PACK)]
+        for t in range(PACK):
+            nc.scalar.copy(h_win[t][:, 0:HALF], h_acc[0][t][:])
+
+        def fetch_h(t):
+            part = parts[t]
+            nc.scalar.copy(h_win[t][:, HALF:S], h_acc[1][t][:])
+            nc.scalar.activation(part[:, 0, :], h_win[t][:].indirect(n5_t[:]), COPY)
+            if t == 0:
+                nc.vector.tensor_scalar(part[:, 1, :], h_win[t][:].indirect(n6_t[:]), -1.0, 0.0, ALU.mult, ALU.add)
+            else:
+                nc.scalar.activation(part[:, 1, :], h_win[t][:].indirect(n6_t[:]), COPY, scale=-1.0)
+            nc.scalar.activation(part[:, 2, :], part[:, 0, :], COPY, scale=0.75)
+            nc.scalar.activation(part[:, 3, :], part[:, 1, :], COPY, scale=-0.75)
+
+        def put_difference(t):
+            nc.vector.tensor_tensor(placed[t][:].indirect(n6_t[:]), parts[t][:, 0, :], parts[t][:, 1, :], ALU.add)
+
+        def put_sum(t):
+            nc.vector.tensor_tensor(placed[t][:].indirect(n5_t[:]), parts[t][:, 2, :], parts[t][:, 3, :], ALU.add)
+            nc.sync.dma_start(out_rows[:, t, :], placed[t][:])
+
+        for t in range(PACK):
+            fetch_h(t)
+        for t in range(PACK):
+            put_difference(t)
+            if t > 0:
+                put_sum(t - 1)
+                nc.scalar.copy(y_rows[:, t - 1, :], placed[t - 1][:])
+        put_sum(PACK - 1)
+        nc.vector.tensor_copy(y_rows[:, PACK - 1, :], placed[PACK - 1][:])
+
+        y_bf = keep.tile([P, S, PACK], BF16, name="y_bf", align_bytes=64)
+        y_words = keep.tile([P, S], U32, name="y_words", align_bytes=64)
+        y_plane = keep.tile([P, S], U8, name="y_plane", align_bytes=64)
+        for h, copy in ((0, nc.vector.tensor_copy), (1, nc.scalar.copy)):
+            cols = slice(h * HALF, (h + 1) * HALF)
+            copy(
+                y_bf[:, cols, :].rearrange("p (c i) t -> p c t i", i=4),
+                y_rows[:, :, cols].rearrange("p t (c i) -> p c t i", i=4),
+            )
+        for h in range(2):
+            cols = slice(h * HALF, (h + 1) * HALF)
+            nc.vector.quantize_mx(
+                out=y_words[:, cols].bitcast(FP8X4), scales=y_plane[:, cols],
+                in_=y_bf[:, cols, :].rearrange("p j t -> p (j t)"),
+            )
+        nc.sync.dma_start(out_1[0].rearrange("p n r -> p (n r)").bitcast(I32), y_words[:].bitcast(I32))
+        for q in range(4):
+            queue = nc.scalar if q % 2 else nc.sync
+            queue.dma_start(out_2[0, 4 * q : 4 * q + 4, :].bitcast(I32), y_plane[32 * q : 32 * q + 4, :].bitcast(I32))

@@ -41,22 +41,22 @@ def tile_picked_twpqpathbhaar_none_po_kernel(
             nc.sync.dma_start(tile[:].bitcast(I32), dram[0].rearrange("p n r -> p (n r)").bitcast(I32))
             return tile
 
-        def load_scale_window(name, dram):
+        def load_scale_window(name, dram, engine):
             tile = keep.tile([P, dram.shape[2]], U8, name=name, align_bytes=64)
-            nc.vector.memset(tile[:].bitcast(I32), 0)
+            engine.memset(tile[:].bitcast(I32), 0)
             nc.sync.dma_start(tile[0:P:8, :].bitcast(I32), dram[0].bitcast(I32))
             return tile
 
         k1_t = load_list("k1_t", k1)
-        ds_win = load_scale_window("ds_win", d_scales)
         offs_t = load_list("offs_t", offs)
-        xs_win = load_scale_window("xs_win", x_scales)
+        ds_win = load_scale_window("ds_win", d_scales, nc.gpsimd)
+        xs_win = load_scale_window("xs_win", x_scales, nc.vector)
         xw_win = load_words("xw_win", x_words)
         dw_win = load_words("dw_win", d_words)
-        k2_t = load_list("k2_t", k2)
-        two_t = load_list("two_t", two)
         gain = keep.tile([P, PACK], F32, name="gain")
         nc.sync.dma_start(gain[:], gn.rearrange("(p t) o -> p (t o)", t=PACK))
+        k2_t = load_list("k2_t", k2)
+        two_t = load_list("two_t", two)
         n1_t = load_list("n1_t", n1)
         n2_t = load_list("n2_t", n2)
         n3_t = load_list("n3_t", n3)
@@ -70,21 +70,20 @@ def tile_picked_twpqpathbhaar_none_po_kernel(
                 src.rearrange("p (c i t) -> p c t i", t=PACK, i=run),
             )
 
-        def pick(name, d_list, x_list, queue):
-            ds = keep.tile([P, H], U8, name=name + "_ds", align_bytes=64)
-            xs = keep.tile([P, S], U8, name=name + "_xs", align_bytes=64)
+        def pick(name, d_list, x_list, queue, picked_tag):
+            picked = keep.tile([P, H + S], U8, name=name + "_picked", tag=picked_tag, align_bytes=64)
             planes = keep.tile([P, H + S], U8, name=name + "_planes", align_bytes=64)
-            nc.vector.tensor_copy(ds[:], ds_win[:].indirect(d_list[:]))
-            nc.vector.tensor_copy(xs[:], xs_win[:].indirect(x_list[:]))
-            deal(nc.vector, planes[:, 0:H], ds[:], 16)
-            nc.vector.tensor_copy(planes[:, H : H + S].bitcast(I32), xs[:].bitcast(I32))
+            nc.vector.tensor_copy(picked[:, 0:H], ds_win[:].indirect(d_list[:]))
+            nc.vector.tensor_copy(picked[:, H : H + S], xs_win[:].indirect(x_list[:]))
+            deal(nc.vector, planes[:, 0:H], picked[:, 0:H], 16)
+            nc.vector.tensor_copy(planes[:, H : H + S].bitcast(I32), picked[:, H : H + S].bitcast(I32))
             for s in range(1, 4):
                 queue.dma_start(planes[s:P:32, :].bitcast(I32), planes[8 * s : P : 32, :].bitcast(I32))
-            xw = keep.tile([P, S], U32, name=name + "_xw", align_bytes=64)
-            dw = keep.tile([P, H], U32, name=name + "_dw", align_bytes=64)
+            dw = keep.tile([P, H], U32, name=name + "_dw", tag="undealt", align_bytes=64)
+            xw = keep.tile([P, S], U32, name=name + "_xw", tag="xw", align_bytes=64)
             dealt = keep.tile([P, H], U32, name=name + "_dealt", align_bytes=64)
-            nc.vector.tensor_copy(xw[:], xw_win[:].indirect(x_list[:]))
             nc.vector.tensor_copy(dw[:], dw_win[:].indirect(d_list[:]))
+            nc.vector.tensor_copy(xw[:], xw_win[:].indirect(x_list[:]))
             deal(nc.vector, dealt[:].bitcast(I32), dw[:].bitcast(I32), 4)
             return dealt, planes[:, 0:H], xw[:], planes[:, H : H + S]
 
@@ -102,29 +101,24 @@ def tile_picked_twpqpathbhaar_none_po_kernel(
         nc.scalar.activation(size[:], gain[:], ACT.Abs, scale=0.0625)
         nc.scalar.activation(sign[:], gain[:], ACT.Sign)
 
-        a_ops = pick("a", k1_t, offs_t, nc.scalar)
+        a_ops = pick("a", k1_t, offs_t, nc.scalar, "a_picked")
         a_acc = [product(t, t, *a_ops) for t in range(PACK)]
-        b_ops = pick("b", k2_t, two_t, nc.sync)
+        b_ops = pick("b", k2_t, two_t, nc.sync, "undealt")
         b_acc = [product(PACK + t, t, *b_ops) for t in range(PACK)]
 
-        w_raw = keep.tile([P, N], U32, name="w_raw", tag="a_dw", align_bytes=64)
+        w_raw = keep.tile([P, N], U32, name="w_raw", align_bytes=64)
         nc.sync.dma_start(w_raw[:].bitcast(I32), w1_words[0].rearrange("p n r -> p (n r)").bitcast(I32))
-        ws_raw = keep.tile([P, N], U8, name="ws_raw", tag="a_xs", align_bytes=64)
+        ws_raw = keep.tile([P, N], U8, name="ws_raw", tag="a_picked", align_bytes=64)
         nc.gpsimd.memset(ws_raw[:].bitcast(I32), 0)
         for q in range(4):
             nc.sync.dma_start(ws_raw[32 * q : 32 * q + 4, :].bitcast(I32), w1_scales[0, 4 * q : 4 * q + 4, :].bitcast(I32))
-        w_dealt = keep.tile([P, N], U32, name="w_dealt", align_bytes=64)
-        ws_dealt = keep.tile([P, N], U8, name="ws_dealt", align_bytes=64)
+        w_dealt = keep.tile([P, N], U32, name="w_dealt", tag="a_dealt", align_bytes=64)
+        ws_dealt = keep.tile([P, N], U8, name="ws_dealt", tag="a_planes", align_bytes=64)
         deal(nc.vector, w_dealt[:].bitcast(I32), w_raw[:].bitcast(I32), 4)
         deal(nc.vector, ws_dealt[:], ws_raw[:], 16)
 
-        def evacuate(name, acc, t):
-            win = keep.tile([P, S], F32, name=name)
-            nc.scalar.activation(win[:], acc[:], COPY, scale=size[:, t : t + 1])
-            return win
-
-        from_a = [keep.tile([P, 2, PACK, HALF], F32, name="from_a%d" % h) for h in range(2)]
-        from_b = keep.tile([P, 2, PACK, HALF], F32, name="from_b")
+        from_a = keep.tile([P, 2, PACK, S], F32, name="from_a")
+        from_b = [keep.tile([P, 2, PACK, HALF], F32, name="from_b%d" % h) for h in range(2)]
         sums = [keep.tile([P, 2, PACK, HALF], F32, name="sums%d" % h) for h in range(2)]
         z_pairs = [keep.tile([P, 2, HALF, 2], BF16, name="z_pairs%d" % h, align_bytes=64) for h in range(2)]
         z_bf = [keep.tile([P, HALF, 2, 2], BF16, name="z_bf%d" % h, align_bytes=64) for h in range(2)]
@@ -133,19 +127,22 @@ def tile_picked_twpqpathbhaar_none_po_kernel(
         a_lists = (n1_t, n2_t)
         b_lists = (n3_t, n4_t)
 
-        def fetch(dst, win, which, h, t):
+        def fetch_a(t):
             for u in range(2):
-                nc.scalar.activation(dst[:, u, t, :], win[t][:].indirect(which[u][:, h * 16 : (h + 1) * 16]), COPY)
+                nc.scalar.activation(from_a[:, u, t, :], a_win[t][:].indirect(a_lists[u][:]), COPY)
 
-        def fetch_b_and_add(h, t):
-            for u in range(2):
-                nc.vector.tensor_tensor(
-                    sums[h][:, u, t, :], b_win[t][:].indirect(b_lists[u][:, h * 16 : (h + 1) * 16]),
-                    from_a[h][:, u, t, :], ALU.add,
-                )
+        def fetch_b(h, t, u):
+            nc.scalar.activation(from_b[h][:, u, t, :], b_win[t][:].indirect(b_lists[u][:, 16 * h : 16 * h + 16]), COPY)
 
-        def add(h, t):
-            nc.vector.tensor_tensor(sums[h][:, :, t, :], from_b[:, :, t, :], from_a[h][:, :, t, :], ALU.add)
+        def fetch_b_and_add(t, u):
+            nc.vector.tensor_tensor(
+                sums[0][:, u, t, :], b_win[t][:].indirect(b_lists[u][:, 0:16]), from_a[:, u, t, 0:HALF], ALU.add
+            )
+
+        def add(h, t, which):
+            nc.vector.tensor_tensor(
+                sums[h][:, which, t, :], from_b[h][:, which, t, :], from_a[:, which, t, h * HALF : (h + 1) * HALF], ALU.add
+            )
 
         def larger(h, pair):
             rows = slice(2 * pair, 2 * pair + 2)
@@ -166,32 +163,36 @@ def tile_picked_twpqpathbhaar_none_po_kernel(
             )
             return [product(PACK * h + t, t, w_dealt, ws_dealt[:], z_words[h][:], z_plane[h][:]) for t in range(PACK)]
 
-        a_win = [evacuate("a_win%d" % t, a_acc[t], t) for t in range(PACK)]
-        fetch(from_a[0], a_win, a_lists, 0, 0)
-        fetch(from_a[0], a_win, a_lists, 0, 1)
-        b_win = [evacuate("b_win%d" % t, b_acc[t], t) for t in range(2)]
-        fetch(from_a[0], a_win, a_lists, 0, 2)
-        b_win.append(evacuate("b_win2", b_acc[2], 2))
-        fetch(from_a[0], a_win, a_lists, 0, 3)
-        b_win.append(evacuate("b_win3", b_acc[3], 3))
+        a_win = [keep.tile([P, 2 * S], F32, name="a_win%d" % t) for t in range(PACK)]
+        b_win = [keep.tile([P, S], F32, name="b_win%d" % t) for t in range(PACK)]
         for t in range(PACK):
-            fetch(from_a[1], a_win, a_lists, 1, t)
-        for t in range(1, PACK):
-            fetch(from_b, b_win, b_lists, 1, t)
+            nc.gpsimd.memset(a_win[t][:, S : 2 * S], 0.0)
+            nc.scalar.activation(a_win[t][:, 0:S], a_acc[t][:], COPY, scale=size[:, t : t + 1])
+        for t in range(PACK):
+            nc.vector.tensor_scalar(b_win[t][:], b_acc[t][:], size[:, t : t + 1], None, ALU.mult)
+        for t in range(PACK):
+            fetch_a(t)
+        fetch_b(0, 0, 0)
+        for t in range(PACK):
+            for u in range(2):
+                fetch_b(1, t, u)
 
-        fetch_b_and_add(0, 0)
-        fetch_b_and_add(0, 1)
-        fetch_b_and_add(0, 2)
-        larger(0, 0)
-        fetch_b_and_add(0, 3)
-        fetch_b_and_add(1, 0)
+        both = slice(0, 2)
+        for t in range(PACK):
+            for u in range(2):
+                if (t, u) != (0, 0):
+                    fetch_b_and_add(t, u)
+        add(0, 0, slice(0, 1))
         larger(0, 1)
-        add(1, 1)
+        larger(0, 0)
+        add(1, 0, both)
+        add(1, 1, both)
         sign_z(0)
         larger(1, 0)
+        add(1, 2, both)
+        add(1, 3, slice(0, 1))
+        add(1, 3, slice(1, 2))
         h_acc = [quantise_z(0)]
-        add(1, 2)
-        add(1, 3)
         larger(1, 1)
         sign_z(1)
         h_acc.append(quantise_z(1))
@@ -212,8 +213,10 @@ def tile_picked_twpqpathbhaar_none_po_kernel(
                 nc.vector.tensor_scalar(part[:, 1, :], h_win[t][:].indirect(n6_t[:]), -1.0, 0.0, ALU.mult, ALU.add)
             else:
                 nc.scalar.activation(part[:, 1, :], h_win[t][:].indirect(n6_t[:]), COPY, scale=-1.0)
-            nc.scalar.activation(part[:, 2, :], part[:, 0, :], COPY, scale=0.75)
-            nc.scalar.activation(part[:, 3, :], part[:, 1, :], COPY, scale=-0.75)
+
+        def scale_pair(t):
+            nc.scalar.activation(parts[t][:, 2, :], parts[t][:, 0, :], COPY, scale=0.75)
+            nc.scalar.activation(parts[t][:, 3, :], parts[t][:, 1, :], COPY, scale=-0.75)
 
         def put_difference(t):
             nc.vector.tensor_tensor(placed[t][:].indirect(n6_t[:]), parts[t][:, 0, :], parts[t][:, 1, :], ALU.add)
@@ -224,6 +227,9 @@ def tile_picked_twpqpathbhaar_none_po_kernel(
 
         for t in range(PACK):
             fetch_h(t)
+            if t > 0:
+                scale_pair(t - 1)
+        scale_pair(PACK - 1)
         for t in range(PACK):
             put_difference(t)
             if t > 0:
@@ -247,7 +253,7 @@ def tile_picked_twpqpathbhaar_none_po_kernel(
                 out=y_words[:, cols].bitcast(FP8X4), scales=y_plane[:, cols],
                 in_=y_bf[:, cols, :].rearrange("p j t -> p (j t)"),
             )
-        nc.sync.dma_start(out_1[0].rearrange("p n r -> p (n r)").bitcast(I32), y_words[:].bitcast(I32))
+            nc.sync.dma_start(out_1[0].rearrange("p n r -> p (n r)").bitcast(I32)[:, cols], y_words[:, cols].bitcast(I32))
         for q in range(4):
             queue = nc.scalar if q % 2 else nc.sync
             queue.dma_start(out_2[0, 4 * q : 4 * q + 4, :].bitcast(I32), y_plane[32 * q : 32 * q + 4, :].bitcast(I32))

@@ -49,7 +49,7 @@ def tile_picked_twpqpathbhaar_none_po_kernel(
 
         k1_t = load_list("k1_t", k1)
         offs_t = load_list("offs_t", offs)
-        ds_win = load_scale_window("ds_win", d_scales, nc.gpsimd)
+        ds_win = load_scale_window("ds_win", d_scales, nc.vector)
         xs_win = load_scale_window("xs_win", x_scales, nc.vector)
         xw_win = load_words("xw_win", x_words)
         dw_win = load_words("dw_win", d_words)
@@ -96,6 +96,12 @@ def tile_picked_twpqpathbhaar_none_po_kernel(
             )
             return acc
 
+        a_win = [keep.tile([P, 2 * S], F32, name="a_win%d" % t) for t in range(PACK)]
+        zero = keep.tile([P, 1], F32, name="zero")
+        nc.vector.memset(zero[:], 0.0)
+        for t in range(PACK):
+            nc.scalar.copy(a_win[t][:, S : 2 * S], zero[:].to_broadcast([P, S]))
+
         size = keep.tile([P, PACK], F32, name="size")
         sign = keep.tile([P, PACK], BF16, name="sign")
         nc.scalar.activation(size[:], gain[:], ACT.Abs, scale=0.0625)
@@ -108,8 +114,8 @@ def tile_picked_twpqpathbhaar_none_po_kernel(
 
         w_raw = keep.tile([P, N], U32, name="w_raw", align_bytes=64)
         nc.sync.dma_start(w_raw[:].bitcast(I32), w1_words[0].rearrange("p n r -> p (n r)").bitcast(I32))
-        ws_raw = keep.tile([P, N], U8, name="ws_raw", tag="a_picked", align_bytes=64)
-        nc.gpsimd.memset(ws_raw[:].bitcast(I32), 0)
+        ws_raw = keep.tile([P, N], U8, name="ws_raw", align_bytes=64)
+        nc.vector.memset(ws_raw[:].bitcast(I32), 0)
         for q in range(4):
             nc.sync.dma_start(ws_raw[32 * q : 32 * q + 4, :].bitcast(I32), w1_scales[0, 4 * q : 4 * q + 4, :].bitcast(I32))
         w_dealt = keep.tile([P, N], U32, name="w_dealt", tag="a_dealt", align_bytes=64)
@@ -163,10 +169,8 @@ def tile_picked_twpqpathbhaar_none_po_kernel(
             )
             return [product(PACK * h + t, t, w_dealt, ws_dealt[:], z_words[h][:], z_plane[h][:]) for t in range(PACK)]
 
-        a_win = [keep.tile([P, 2 * S], F32, name="a_win%d" % t) for t in range(PACK)]
         b_win = [keep.tile([P, S], F32, name="b_win%d" % t) for t in range(PACK)]
         for t in range(PACK):
-            nc.gpsimd.memset(a_win[t][:, S : 2 * S], 0.0)
             nc.scalar.activation(a_win[t][:, 0:S], a_acc[t][:], COPY, scale=size[:, t : t + 1])
         for t in range(PACK):
             nc.vector.tensor_scalar(b_win[t][:], b_acc[t][:], size[:, t : t + 1], None, ALU.mult)

from contextlib import ExitStack

import concourse.mybir as mybir

K, T, S, N, G, H, W = 512, 1024, 512, 512, 2048, 512, 256
FLOPS = 3 * 2 * 512 * 512 * 512

F32 = mybir.dt.float32
BF16 = mybir.dt.bfloat16
I32 = mybir.dt.int32
U32 = mybir.dt.uint32
U16 = mybir.dt.uint16
U8 = mybir.dt.uint8
FP8X4 = mybir.dt.float8_e4m3fn_x4
ALU = mybir.AluOpType
ACT = mybir.ActivationFunctionType
COPY = ACT.Copy

P = 128
PACK = 4
HALF = 256


def tile_picked_twpqpathbhaar_none_po_kernel(
    tc, x_words, x_scales, d_words, d_scales, gn, w1_words, w1_scales,
    offs, k1, two, k2, n1, n2, n3, n4, n5, n6, out_0, out_1, out_2,
):
    nc = tc.nc
    with ExitStack() as ctx:
        lists = ctx.enter_context(tc.tile_pool(name="lists", bufs=1))
        keep = ctx.enter_context(tc.tile_pool(name="keep", bufs=1))
        psum = ctx.enter_context(tc.psum_pool(name="psum", bufs=1))

        def load_list(name, dram):
            tile = lists.tile(list(dram.shape), U16, name=name)
            nc.sync.dma_start(tile[:], dram)
            return tile

        def load_words(name, dram):
            tile = keep.tile([P, dram.shape[2]], U32, name=name, align_bytes=64)
            nc.sync.dma_start(tile[:].bitcast(I32), dram[0].rearrange("p n r -> p (n r)").bitcast(I32))
            return tile

        def load_scale_window(name, dram, engine):
            tile = keep.tile([P, dram.shape[2]], U8, name=name, align_bytes=64)
            engine.memset(tile[:].bitcast(I32), 0)
            nc.sync.dma_start(tile[0:P:8, :].bitcast(I32), dram[0].bitcast(I32))
            return tile

        k1_t = load_list("k1_t", k1)
        offs_t = load_list("offs_t", offs)
        ds_win = load_scale_window("ds_win", d_scales, nc.vector)
        xs_win = load_scale_window("xs_win", x_scales, nc.vector)
        xw_win = load_words("xw_win", x_words)
        dw_win = load_words("dw_win", d_words)
        gain = keep.tile([P, PACK], F32, name="gain")
        nc.sync.dma_start(gain[:], gn.rearrange("(p t) o -> p (t o)", t=PACK))
        k2_t = load_list("k2_t", k2)
        two_t = load_list("two_t", two)
        n1_t = load_list("n1_t", n1)
        n2_t = load_list("n2_t", n2)
        n3_t = load_list("n3_t", n3)
        n4_t = load_list("n4_t", n4)
        n5_t = load_list("n5_t", n5)
        n6_t = load_list("n6_t", n6)

        def deal(engine, dst, src, run):
            engine.tensor_copy(
                dst.rearrange("p (t c i) -> p c t i", t=PACK, i=run),
                src.rearrange("p (c i t) -> p c t i", t=PACK, i=run),
            )

        def pick(name, d_list, x_list, queue, picked_tag):
            picked = keep.tile([P, H + S], U8, name=name + "_picked", tag=picked_tag, align_bytes=64)
            planes = keep.tile([P, H + S], U8, name=name + "_planes", align_bytes=64)
            nc.vector.tensor_copy(picked[:, 0:H], ds_win[:].indirect(d_list[:]))
            nc.vector.tensor_copy(picked[:, H : H + S], xs_win[:].indirect(x_list[:]))
            deal(nc.vector, planes[:, 0:H], picked[:, 0:H], 16)
            nc.vector.tensor_copy(planes[:, H : H + S].bitcast(I32), picked[:, H : H + S].bitcast(I32))
            for s in range(1, 4):
                queue.dma_start(planes[s:P:32, :].bitcast(I32), planes[8 * s : P : 32, :].bitcast(I32))
            dw = keep.tile([P, H], U32, name=name + "_dw", tag="undealt", align_bytes=64)
            xw = keep.tile([P, S], U32, name=name + "_xw", tag="xw", align_bytes=64)
            dealt = keep.tile([P, H], U32, name=name + "_dealt", align_bytes=64)
            nc.vector.tensor_copy(dw[:], dw_win[:].indirect(d_list[:]))
            nc.vector.tensor_copy(xw[:], xw_win[:].indirect(x_list[:]))
            deal(nc.vector, dealt[:].bitcast(I32), dw[:].bitcast(I32), 4)
            return dealt, planes[:, 0:H], xw[:], planes[:, H : H + S]

        def product(bank, t, lhs_words, lhs_plane, rhs_words, rhs_plane):
            acc = psum.tile([P, rhs_words.shape[1]], F32, name="acc", tag="bank%d" % bank)
            cols = slice(t * P, (t + 1) * P)
            nc.tensor.matmul_mx(
                out=acc[:], lhsT=lhs_words[:, cols].bitcast(FP8X4), lhsT_scale=lhs_plane[:, cols],
                rhs=rhs_words.bitcast(FP8X4), rhs_scale=rhs_plane, start=True, stop=True,
            )
            return acc

        a_win = [keep.tile([P, 2 * S], F32, name="a_win%d" % t) for t in range(PACK)]
        zero = keep.tile([P, 1], F32, name="zero")
        nc.vector.memset(zero[:], 0.0)
        for t in range(PACK):
            nc.scalar.copy(a_win[t][:, S : 2 * S], zero[:].to_broadcast([P, S]))

        size = keep.tile([P, PACK], F32, name="size")
        sign = keep.tile([P, PACK], BF16, name="sign")
        nc.scalar.activation(size[:], gain[:], ACT.Abs, scale=0.0625)
        nc.scalar.activation(sign[:], gain[:], ACT.Sign)

        a_ops = pick("a", k1_t, offs_t, nc.scalar, "a_picked")
        a_acc = [product(t, t, *a_ops) for t in range(PACK)]
        b_ops = pick("b", k2_t, two_t, nc.sync, "undealt")
        b_acc = [product(PACK + t, t, *b_ops) for t in range(PACK)]

        w_raw = keep.tile([P, N], U32, name="w_raw", align_bytes=64)
        nc.sync.dma_start(w_raw[:].bitcast(I32), w1_words[0].rearrange("p n r -> p (n r)").bitcast(I32))
        ws_raw = keep.tile([P, N], U8, name="ws_raw", align_bytes=64)
        nc.vector.memset(ws_raw[:].bitcast(I32), 0)
        for q in range(4):
            nc.sync.dma_start(ws_raw[32 * q : 32 * q + 4, :].bitcast(I32), w1_scales[0, 4 * q : 4 * q + 4, :].bitcast(I32))
        w_dealt = keep.tile([P, N], U32, name="w_dealt", tag="a_dealt", align_bytes=64)
        ws_dealt = keep.tile([P, N], U8, name="ws_dealt", tag="a_planes", align_bytes=64)
        deal(nc.vector, w_dealt[:].bitcast(I32), w_raw[:].bitcast(I32), 4)
        deal(nc.vector, ws_dealt[:], ws_raw[:], 16)

        from_a = keep.tile([P, 2, PACK, S], F32, name="from_a")
        from_b = [keep.tile([P, 2, PACK, HALF], F32, name="from_b%d" % h) for h in range(2)]
        sums = [keep.tile([P, 2, PACK, HALF], F32, name="sums%d" % h) for h in range(2)]
        z_pairs = [keep.tile([P, 2, HALF, 2], BF16, name="z_pairs%d" % h, align_bytes=64) for h in range(2)]
        z_bf = [keep.tile([P, HALF, 2, 2], BF16, name="z_bf%d" % h, align_bytes=64) for h in range(2)]
        z_words = [keep.tile([P, HALF], U32, name="z_words%d" % h, align_bytes=64) for h in range(2)]
        z_plane = [keep.tile([P, HALF], U8, name="z_plane%d" % h, align_bytes=64) for h in range(2)]
        a_lists = (n1_t, n2_t)
        b_lists = (n3_t, n4_t)

        def fetch_a(t):
            for u in range(2):
                nc.scalar.activation(from_a[:, u, t, :], a_win[t][:].indirect(a_lists[u][:]), COPY)

        def fetch_b(h, t, u):
            nc.scalar.activation(from_b[h][:, u, t, :], b_win[t][:].indirect(b_lists[u][:, 16 * h : 16 * h + 16]), COPY)

        def fetch_b_and_add(t, u):
            nc.vector.tensor_tensor(
                sums[0][:, u, t, :], b_win[t][:].indirect(b_lists[u][:, 0:16]), from_a[:, u, t, 0:HALF], ALU.add
            )

        def add(h, t, which):
            nc.vector.tensor_tensor(
                sums[h][:, which, t, :], from_b[h][:, which, t, :], from_a[:, which, t, h * HALF : (h + 1) * HALF], ALU.add
            )

        def larger(h, pair):
            rows = slice(2 * pair, 2 * pair + 2)
            nc.vector.tensor_tensor(
                z_pairs[h][:, pair, :, :], sums[h][:, 0, rows, :].rearrange("p e j -> p j e"),
                sums[h][:, 1, rows, :].rearrange("p e j -> p j e"), ALU.max,
            )

        def sign_z(h):
            nc.vector.tensor_tensor(
                z_bf[h][:], z_pairs[h][:].rearrange("p u j e -> p j u e"),
                sign[:].rearrange("p (u e) -> p u e", e=2).unsqueeze(1).to_broadcast([P, HALF, 2, 2]), ALU.mult,
            )

        def quantise_z(h):
            nc.vector.quantize_mx(
                out=z_words[h][:].bitcast(FP8X4), scales=z_plane[h][:], in_=z_bf[h][:].rearrange("p j u e -> p (j u e)")
            )
            return [product(PACK * h + t, t, w_dealt, ws_dealt[:], z_words[h][:], z_plane[h][:]) for t in range(PACK)]

        b_win = [keep.tile([P, S], F32, name="b_win%d" % t) for t in range(PACK)]
        for t in range(PACK):
            nc.scalar.activation(a_win[t][:, 0:S], a_acc[t][:], COPY, scale=size[:, t : t + 1])
        for t in range(PACK):
            nc.vector.tensor_scalar(b_win[t][:], b_acc[t][:], size[:, t : t + 1], None, ALU.mult)
        for t in range(PACK):
            fetch_a(t)
        fetch_b(0, 0, 0)
        for t in range(PACK):
            for u in range(2):
                fetch_b(1, t, u)

        both = slice(0, 2)
        for t in range(PACK):
            for u in range(2):
                if (t, u) != (0, 0):
                    fetch_b_and_add(t, u)
        add(0, 0, slice(0, 1))
        larger(0, 1)
        larger(0, 0)
        add(1, 0, both)
        add(1, 1, both)
        sign_z(0)
        larger(1, 0)
        add(1, 2, both)
        add(1, 3, slice(0, 1))
        add(1, 3, slice(1, 2))
        h_acc = [quantise_z(0)]
        larger(1, 1)
        sign_z(1)
        h_acc.append(quantise_z(1))

        out_rows = out_0.rearrange("(p t) j -> p t j", t=PACK)
        y_rows = keep.tile([P, PACK, S], BF16, name="y_rows", align_bytes=64)
        placed = [keep.tile([P, S], F32, name="placed%d" % t) for t in range(PACK)]
        h_win = [keep.tile([P, S], F32, name="h_win%d" % t) for t in range(PACK)]
        parts = [keep.tile([P, 4, W], F32, name="part%d" % t) for t in range(PACK)]
        for t in range(PACK):
            nc.scalar.copy(h_win[t][:, 0:HALF], h_acc[0][t][:])

        def fetch_h(t):
            part = parts[t]
            nc.scalar.copy(h_win[t][:, HALF:S], h_acc[1][t][:])
            nc.scalar.activation(part[:, 0, :], h_win[t][:].indirect(n5_t[:]), COPY)
            if t == 0:
                nc.vector.tensor_scalar(part[:, 1, :], h_win[t][:].indirect(n6_t[:]), -1.0, 0.0, ALU.mult, ALU.add)
            else:
                nc.scalar.activation(part[:, 1, :], h_win[t][:].indirect(n6_t[:]), COPY, scale=-1.0)

        def scale_pair(t):
            nc.scalar.activation(parts[t][:, 2, :], parts[t][:, 0, :], COPY, scale=0.75)
            nc.scalar.activation(parts[t][:, 3, :], parts[t][:, 1, :], COPY, scale=-0.75)

        def put_difference(t):
            nc.vector.tensor_tensor(placed[t][:].indirect(n6_t[:]), parts[t][:, 0, :], parts[t][:, 1, :], ALU.add)

        def put_sum(t):
            nc.vector.tensor_tensor(placed[t][:].indirect(n5_t[:]), parts[t][:, 2, :], parts[t][:, 3, :], ALU.add)
            nc.sync.dma_start(out_rows[:, t, :], placed[t][:])

        for t in range(PACK):
            fetch_h(t)
            if t > 0:
                scale_pair(t - 1)
        scale_pair(PACK - 1)
        for t in range(PACK):
            put_difference(t)
            if t > 0:
                put_sum(t - 1)
                nc.scalar.copy(y_rows[:, t - 1, :], placed[t - 1][:])
        put_sum(PACK - 1)
        nc.vector.tensor_copy(y_rows[:, PACK - 1, :], placed[PACK - 1][:])

        y_bf = keep.tile([P, S, PACK], BF16, name="y_bf", align_bytes=64)
        y_words = keep.tile([P, S], U32, name="y_words", align_bytes=64)
        y_plane = keep.tile([P, S], U8, name="y_plane", align_bytes=64)
        for h, copy in ((0, nc.vector.tensor_copy), (1, nc.scalar.copy)):
            cols = slice(h * HALF, (h + 1) * HALF)
            copy(
                y_bf[:, cols, :].rearrange("p (c i) t -> p c t i", i=4),
                y_rows[:, :, cols].rearrange("p t (c i) -> p c t i", i=4),
            )
        for h in range(2):
            cols = slice(h * HALF, (h + 1) * HALF)
            nc.vector.quantize_mx(
                out=y_words[:, cols].bitcast(FP8X4), scales=y_plane[:, cols],
                in_=y_bf[:, cols, :].rearrange("p j t -> p (j t)"),
            )
            nc.sync.dma_start(out_1[0].rearrange("p n r -> p (n r)").bitcast(I32)[:, cols], y_words[:, cols].bitcast(I32))
        for q in range(4):
            queue = nc.scalar if q % 2 else nc.sync
            queue.dma_start(out_2[0, 4 * q : 4 * q + 4, :].bitcast(I32), y_plane[32 * q : 32 * q + 4, :].bitcast(I32))
